import numpy as np
import ml_dtypes


def mxq(x, axis, fmt="e4m3"):
    dtype, down = {"e4m3": (ml_dtypes.float8_e4m3fn, 7), "e5m2": (ml_dtypes.float8_e5m2, 14)}[fmt]
    v = np.moveaxis(np.asarray(x, np.float32).astype(ml_dtypes.bfloat16).astype(np.float64), axis, -1)
    blocks = v.reshape(v.shape[:-1] + (-1, 32))
    amax = np.abs(blocks).max(-1, keepdims=True)
    byte = np.maximum(np.where(amax > 0, np.frexp(amax)[1] - 1 + 127, 0) - down, 1)
    scale = np.exp2(byte - 127.0)
    codes = (blocks / scale).astype(np.float32).astype(dtype).astype(np.float64)
    return np.moveaxis((codes * scale).reshape(v.shape), -1, axis)


WIDE = False


def mx_kscale(k):
    if not WIDE:
        return np.ones(k)
    levels = np.array([10, -10, 5, -5, 0])
    if k % 512:
        return np.exp2(np.random.permutation(np.resize(levels, k // 32))).repeat(32)
    a = np.empty((k // 512, 16))
    for p in range(k // 512):
        a[p, :8] = np.random.permutation(np.resize(levels, 8))
        for g in range(8):
            far = levels[np.abs(levels - a[p, g]) >= 10]
            a[p, g + 8] = far[np.random.randint(len(far))]
    return np.exp2(a.ravel()).repeat(32)


def f64(x):
    return np.asarray(x).astype(np.float64)


def striped(idx):
    return np.tile(np.asarray(idx).reshape(-1, 16).T, (8, 1)).astype(np.uint16)


def unstriped(offs):
    return offs[:16].T.reshape(-1).astype(np.int64)


E2M1 = np.array([0.0, 0.5, 1.0, 1.5, 2.0, 3.0, 4.0, 6.0, -0.0, -0.5, -1.0, -1.5, -2.0, -3.0, -4.0, -6.0])


def pack_weight(w, fmt):
    k, n = w.shape
    w = f64(np.asarray(w, np.float32).astype(ml_dtypes.bfloat16)).reshape(k // 32, 32, n)
    amax = np.abs(w).max(1)
    if fmt == "e4m3":
        byte = np.frexp(amax)[1] - 1 + 127 - 7
    else:
        mant, ex = np.frexp(amax / 6.0)
        byte = np.where(mant > 0.5, ex, ex - 1) + 127
    byte = np.clip(np.where(amax > 0, byte, 1), 1, 254)
    scaled = (w * np.exp2(127.0 - byte)[:, None, :]).reshape(k, n).astype(np.float32)
    by_word = np.ascontiguousarray(scaled.reshape(k // 512, 128, 4, n).transpose(0, 1, 3, 2))
    if fmt == "e4m3":
        words = by_word.astype(ml_dtypes.float8_e4m3fn).view(np.uint8)
    else:
        c = by_word.astype(ml_dtypes.float4_e2m1fn).view(np.uint8) & 0xF
        words = (c[..., 0::2] | (c[..., 1::2] << 4)).reshape(k // 512, 128, 2 * n)
    return np.ascontiguousarray(words), np.ascontiguousarray(byte.astype(np.uint8).reshape(k // 512, 16, n))


def unpack_weight(words, scales, fmt):
    g, _, n = scales.shape
    words = np.ascontiguousarray(words).reshape(g, 128, n, -1)
    if fmt == "e4m3":
        vals = words.view(ml_dtypes.float8_e4m3fn).astype(np.float64)
    else:
        nib = np.empty((g, 128, n, 4), np.uint8)
        nib[..., 0::2] = words & 0xF
        nib[..., 1::2] = words >> 4
        vals = E2M1[nib]
    vals = vals * np.repeat(np.exp2(scales.astype(np.float64) - 127.0), 8, axis=1)[..., None]
    return vals.transpose(0, 1, 3, 2).reshape(g * 512, n)


D, E, T, I, Q, G = 512, 512, 2048, 512, 128, 64


def setup_inputs():
    n = np.random.standard_normal
    idx = np.random.permutation(T)[:I]
    fd = mx_kscale(D)
    fe = mx_kscale(E)
    keysp = pack_weight(n((D, T)) / fd[:, None], "e2m1")
    valsp = pack_weight(n((E, T)) / fe[:, None], "e2m1")
    return {
        "query": (n((D, Q)) * 1.0 / np.sqrt(D) * fd[:, None]).astype(np.float32),
        "keys_words": keysp[0],
        "keys_scales": keysp[1],
        "cv1": np.tile(np.random.uniform(0.3, 1.5, T), (128, 1)).astype(np.float32),
        "cv2": np.tile(np.random.uniform(-0.5, 0.3, T), (128, 1)).astype(np.float32),
        "shy": (np.random.uniform(20.0, 60.0, (Q, 1))).astype(np.float32),
        "gout": (n((E, Q)) * 1 / np.sqrt(E) * fe[:, None]).astype(np.float32),
        "vals_words": valsp[0],
        "vals_scales": valsp[1],
        "dquery": (n((D, Q)) * 1.0 / np.sqrt(D) * fd[:, None]).astype(np.float32),
        "base": (0.5 * n((Q, T))).astype(np.float32),
        "offs": striped(idx),
    }


def reference(query, keys_words, keys_scales, cv1, cv2, shy, gout, vals_words, vals_scales, dquery, base, offs):
    idx = unstriped(offs)
    keysu = unpack_weight(keys_words, keys_scales, "e2m1")
    valsu = unpack_weight(vals_words, vals_scales, "e2m1")
    queryq = mxq(f64(query), 0, "e4m3")
    keysidxg = keysu[:, idx]
    a = queryq.T @ keysidxg
    dqueryq = mxq(f64(dquery), 0, "e4m3")
    ta = dqueryq.T @ keysidxg
    s = a * f64(cv1)[:1][:, idx] + np.square(a) * f64(cv2)[:1][:, idx]
    p = np.exp(s - np.max(s, axis=1, keepdims=True))
    r = p / np.sum(p, axis=1, keepdims=True)
    pg = r.reshape(Q, G, I // G).sum(axis=2)
    k0 = np.exp(pg * f64(shy) * (-1.0))
    kr = np.repeat(k0, I // G, axis=1)
    u0 = r * kr
    goutq = mxq(f64(gout), 0, "e4m3")
    valsidxg = valsu[:, idx]
    c0 = goutq.T @ valsidxg
    du0 = c0 / np.sum(u0, axis=1, keepdims=True) + np.sum(c0 * u0 / np.square(np.sum(u0, axis=1, keepdims=True)) * (-1.0), axis=1, keepdims=True)
    dkr = du0 * r
    dk0 = dkr.reshape(Q, G, I // G).sum(axis=2)
    dpg = dk0 * k0 * (-1.0) * f64(shy)
    r1 = np.repeat(dpg, I // G, axis=1)
    dr = du0 * kr + r1
    dp = dr / np.sum(p, axis=1, keepdims=True) + np.sum(dr * p / np.square(np.sum(p, axis=1, keepdims=True)) * (-1.0), axis=1, keepdims=True)
    ds = dp * p
    ts = ta * f64(cv1)[:1][:, idx] + ta * a * 2.0 * f64(cv2)[:1][:, idx]
    tp = ts * p
    tr = (tp - np.sum(tp, axis=1, keepdims=True) * p / np.sum(p, axis=1, keepdims=True)) / np.sum(p, axis=1, keepdims=True)
    tpg = tr.reshape(Q, G, I // G).sum(axis=2)
    tk0 = tpg * f64(shy) * (-1.0) * k0
    tkr = np.repeat(tk0, I // G, axis=1)
    tu0 = tr * kr + tkr * r
    tdu0 = np.sum(tu0, axis=1, keepdims=True) * c0 / np.square(np.sum(u0, axis=1, keepdims=True)) * (-1.0) + np.sum((tu0 * c0 - np.sum(tu0, axis=1, keepdims=True) * np.sum(u0, axis=1, keepdims=True) * 2.0 * c0 * u0 / np.square(np.sum(u0, axis=1, keepdims=True))) / np.square(np.sum(u0, axis=1, keepdims=True)) * (-1.0), axis=1, keepdims=True)
    tdkr = tdu0 * r + tr * du0
    tdk0 = tdkr.reshape(Q, G, I // G).sum(axis=2)
    tdpg = (tdk0 * k0 + tk0 * dk0) * (-1.0) * f64(shy)
    tr1 = np.repeat(tdpg, I // G, axis=1)
    tdr = tdu0 * kr + tkr * du0 + tr1
    tdp = (tdr - np.sum(tp, axis=1, keepdims=True) * dr / np.sum(p, axis=1, keepdims=True)) / np.sum(p, axis=1, keepdims=True) + np.sum((tdr * p + tp * dr - np.sum(tp, axis=1, keepdims=True) * np.sum(p, axis=1, keepdims=True) * 2.0 * dr * p / np.square(np.sum(p, axis=1, keepdims=True))) / np.square(np.sum(p, axis=1, keepdims=True)) * (-1.0), axis=1, keepdims=True)
    tds = tdp * p + tp * dp
    tda = tds * f64(cv1)[:1][:, idx] + (tds * f64(cv2)[:1][:, idx] * a + ta * ds * f64(cv2)[:1][:, idx]) * 2.0
    gs = tda * 512.0
    gf = np.zeros((Q, T))
    gf[:, idx] = gs
    y = f64(base) + gf
    return y

@@ -1,0 +1,341 @@
+from contextlib import ExitStack
+
+import concourse.mybir as mybir
+from concourse.masks import make_identity
+
+F32 = mybir.dt.float32
+BF16 = mybir.dt.bfloat16
+I32 = mybir.dt.int32
+U32 = mybir.dt.uint32
+U16 = mybir.dt.uint16
+U8 = mybir.dt.uint8
+FP8X4 = mybir.dt.float8_e4m3fn_x4
+FP4X4 = mybir.dt.float4_e2m1fn_x4
+ALU = mybir.AluOpType
+ACT = mybir.ActivationFunctionType
+AXIS = mybir.AxisListType
+
+P = 128
+D, T, SLOTS, Q = 512, 2048, 512, 128
+RUN = 8
+G = SLOTS // RUN
+BLOCKS = SLOTS // P
+PACK = 4
+OUT_SCALE = 512.0
+STORE_WIDTHS = (256, 512, 512, 512, 256)
+
+FLOPS = 3 * 2 * D * Q * SLOTS
+
+
+def tile_attend_hvowncurve_crowdshy_s_kernel(
+    tc, query, keys_words, keys_scales, cv1, cv2, shy, gout, vals_words, vals_scales, dquery, base, offs, out
+):
+    nc = tc.nc
+    V, S, PE = nc.vector, nc.scalar, nc.tensor
+    mult, add, sub = ALU.mult, ALU.add, ALU.subtract
+
+    with ExitStack() as ctx:
+        sb = ctx.enter_context(tc.tile_pool(name="sb", bufs=1))
+        ps = ctx.enter_context(tc.psum_pool(name="ps", bufs=1))
+
+        def wide(name):
+            return sb.tile([P, SLOTS], F32, name=name)
+
+        def runs(name):
+            return sb.tile([P, G], F32, name=name)
+
+        def column(name):
+            return sb.tile([P, 1], F32, name=name)
+
+        def bank(name, tag):
+            return ps.tile([P, SLOTS], F32, name=name, tag=tag)
+
+        def by_run(ap):
+            return ap.rearrange("p (g j) -> p g j", j=RUN)
+
+        def spread(ap):
+            return ap.unsqueeze(2).to_broadcast([P, G, RUN])
+
+        def block(j):
+            return slice(j * P, (j + 1) * P)
+
+        offsets = sb.tile([P, SLOTS // 16], U16, name="offsets")
+        nc.sync.dma_start(offsets[:], offs)
+
+        def load_scale_rows(name, scales):
+            window = sb.tile([P, T], U8, name=name)
+            V.memset(window[:].bitcast(I32), 0)
+            for quad in range(4):
+                nc.sync.dma_start(
+                    window[32 * quad : 32 * quad + 4, :].bitcast(I32),
+                    scales[0, 4 * quad : 4 * quad + 4, :].bitcast(I32),
+                )
+            return window
+
+        def load_words(name, words, tag):
+            window = sb.tile([P, T], U16, name=name, tag=tag)
+            nc.sync.dma_start(window[:].bitcast(I32), words[0].bitcast(I32))
+            return window
+
+        def load_row(name, table, tag):
+            window = sb.tile([P, T], F32, name=name, tag=tag)
+            V.memset(window[:], 0.0)
+            nc.sync.dma_start(window[0:1, :], table[0:1, :])
+            return window
+
+        def load_rows(name, rows, tag):
+            raw = sb.tile([P, PACK, Q], F32, name=name, tag=tag)
+            nc.sync.dma_start(raw[:], rows.rearrange("(p j) w -> p j w", j=PACK))
+            return raw
+
+        def round_and_interleave(name, raw, tag):
+            grouped = sb.tile([P, Q, PACK], BF16, name=name, tag=tag, align_bytes=64)
+            S.copy(grouped[:], raw[:].rearrange("p j w -> p w j"))
+            return grouped
+
+        def quantise(name, grouped):
+            codes = sb.tile([P, Q], U32, name=name + "_codes", align_bytes=64)
+            scales = sb.tile([P, Q], U8, name=name + "_scales", align_bytes=64)
+            V.quantize_mx(out=codes[:].bitcast(FP8X4), scales=scales[:], in_=grouped[:].rearrange("p w j -> p (w j)"))
+            return codes, scales
+
+        def gather(name, window, dtype, tag):
+            picked = sb.tile([P, SLOTS], dtype, name=name, tag=tag, align_bytes=64)
+            V.tensor_copy(picked[:], window[:].indirect(offsets[:]))
+            return picked
+
+        def turn(target, source, blocks):
+            for j in blocks:
+                PE.transpose(target[:, block(j)], source[:, block(j)], identity[:])
+
+        key_scale_window = load_scale_rows("key_scale_window", keys_scales)
+        query_raw = load_rows("query_raw", query, "pool_buffer")
+        dquery_raw = load_rows("dquery_raw", dquery, "staging")
+        key_word_window = load_words("key_word_window", keys_words, "key_word_window")
+        cv1_window = load_row("cv1_window", cv1, "row_buffer")
+        cv2_window = load_row("cv2_window", cv2, "cv2_window")
+        val_scale_window = load_scale_rows("val_scale_window", vals_scales)
+
+        identity = sb.tile([P, P], F32, name="identity")
+        make_identity(nc, identity[:])
+        shyness = column("shyness")
+        nc.gpsimd.dma_start(shyness[:], shy)
+
+        query_grouped = round_and_interleave("query_grouped", query_raw, "query_grouped")
+        dquery_grouped = round_and_interleave("dquery_grouped", dquery_raw, "dquery_grouped")
+        val_word_window = load_words("val_word_window", vals_words, "pool_buffer")
+        gout_raw = load_rows("gout_raw", gout, "staging")
+
+        key_scales = gather("key_scales", key_scale_window, U8, "key_scales")
+        key_words = gather("key_words", key_word_window, U16, "key_words")
+        query_codes, query_scales = quantise("query", query_grouped)
+
+        cv1_picked = wide("cv1_picked")
+        S.activation(cv1_picked[:], cv1_window[:].indirect(offsets[:]), ACT.Copy)
+        cv1_turned = bank("cv1_turned", "bank0")
+        turn(cv1_turned, cv1_picked, range(BLOCKS))
+        half = SLOTS // 2
+        cv2_turned = []
+        for h in range(2):
+            picked = sb.tile([P, half], F32, name="cv2_picked%d" % h, tag="cv2_picked%d" % h, align_bytes=64)
+            S.activation(picked[:], cv2_window[:].indirect(offsets[:, h * half // 16 : (h + 1) * half // 16]), ACT.Copy)
+            turned = bank("cv2_turned%d" % h, "bank%d" % (1 + h))
+            turn(turned, picked, range(BLOCKS // 2))
+            cv2_turned.append(turned)
+
+        base_sb = sb.tile([P, T], F32, name="base_sb", tag="row_buffer")
+        nc.sync.dma_start(base_sb[:], base)
+        c1 = sb.tile([P, BLOCKS], F32, name="c1")
+        S.copy(c1[:], cv1_turned[:, 0:SLOTS:P])
+
+        def slot_major_product(name, tag, codes, scales):
+            product = bank(name, tag)
+            for j in range(BLOCKS):
+                PE.matmul_mx(
+                    out=product[:, block(j)],
+                    lhsT=key_words[:, block(j)].bitcast(FP4X4),
+                    lhsT_scale=key_scales[:, block(j)],
+                    rhs=codes[:].bitcast(FP8X4),
+                    rhs_scale=scales[:],
+                    start=True,
+                    stop=True,
+                )
+            return product
+
+        a_t = slot_major_product("a_t", "bank3", query_codes, query_scales)
+
+        c2 = sb.tile([P, BLOCKS], F32, name="c2")
+        u_t = sb.tile([P, SLOTS], F32, name="u_t", tag="u_buffer", align_bytes=64)
+        for h in range(2):
+            S.copy(c2[:, 2 * h : 2 * h + 2], cv2_turned[h][:, 0:half:P])
+            for j in (2 * h, 2 * h + 1):
+                S.activation(u_t[:, block(j)], a_t[:, block(j)], ACT.Identity, bias=c1[:, j : j + 1], scale=c2[:, j : j + 1])
+
+        dquery_codes, dquery_scales = quantise("dquery", dquery_grouped)
+        val_scales = gather("val_scales", val_scale_window, U8, "val_scales")
+        ta_t = slot_major_product("ta_t", "bank4", dquery_codes, dquery_scales)
+
+        s_t = wide("s_t")
+        V.tensor_tensor(s_t[:], a_t[:], u_t[:], mult)
+        s = bank("s", "bank6")
+        turn(s, s_t, range(BLOCKS))
+
+        minus_c1 = sb.tile([P, BLOCKS], F32, name="minus_c1")
+        S.activation(minus_c1[:], c1[:], ACT.Copy, scale=-1.0)
+        e_t = wide("e_t")
+        for j in range(BLOCKS):
+            S.activation(e_t[:, block(j)], u_t[:, block(j)], ACT.Identity, bias=minus_c1[:, j : j + 1], scale=2.0)
+        gout_grouped = round_and_interleave("gout_grouped", gout_raw, "cv2_picked1")
+
+        val_words = gather("val_words", val_word_window, U16, "u_buffer")
+        gout_codes, gout_scales = quantise("gout", gout_grouped)
+        c = bank("c", "bank5")
+        PE.matmul_mx(
+            out=c[:],
+            lhsT=gout_codes[:].bitcast(FP8X4),
+            lhsT_scale=gout_scales[:],
+            rhs=val_words[:].bitcast(FP4X4),
+            rhs_scale=val_scales[:],
+            start=True,
+            stop=True,
+        )
+        minus_max = column("minus_max")
+        V.tensor_reduce(minus_max[:], s[:], AXIS.X, ALU.max, negate=True)
+        p = wide("p")
+        p_sum = column("p_sum")
+        S.activation(p[:], s[:], ACT.Exp, bias=minus_max[:], accum_out=p_sum[:])
+
+        scattered = sb.tile([P, T], F32, name="scattered", tag="pool_buffer")
+        nc.gpsimd.memset(scattered[:], 0.0)
+
+        sigma_t = wide("sigma_t")
+        V.tensor_tensor(sigma_t[:], ta_t[:], e_t[:], mult)
+        sigma = bank("sigma", "bank7")
+        turn(sigma, sigma_t, range(BLOCKS))
+
+        e = bank("e", "bank0")
+        turn(e, e_t, range(BLOCKS))
+
+        minus_shy = column("minus_shy")
+        S.activation(minus_shy[:], shyness[:], ACT.Copy, scale=-1.0)
+
+        sums = sb.tile([P, 5, G], F32, name="sums")
+        tan, a0, a1, a2, a3 = [sums[:, n, :] for n in range(5)]
+        inv_s = column("inv_s")
+        V.reciprocal(inv_s[:], p_sum[:])
+        V.tensor_reduce(a0, by_run(p[:]), AXIS.X, add)
+        nh = column("nh")
+        S.activation(nh[:], inv_s[:], ACT.Copy, scale=minus_shy[:])
+        k = runs("k")
+        S.activation(k[:], a0, ACT.Exp, scale=nh[:])
+
+        e_sq = wide("e_sq")
+        S.activation(e_sq[:], e_t[:], ACT.Square)
+        two_c2 = sb.tile([P, BLOCKS], F32, name="two_c2")
+        S.activation(two_c2[:], c2[:], ACT.Copy, scale=2.0)
+        q1_t = wide("q1_t")
+        for j in range(BLOCKS):
+            S.activation(q1_t[:, block(j)], e_sq[:, block(j)], ACT.Identity, bias=two_c2[:, j : j + 1])
+
+        p_sigma = wide("p_sigma")
+        p_sigma_sum = column("p_sigma_sum")
+        V.scalar_tensor_tensor(p_sigma[:], sigma[:], 1.0, p[:], mult, mult, accum_out=p_sigma_sum[:])
+        p_c = wide("p_c")
+        V.tensor_tensor(p_c[:], c[:], p[:], mult)
+        t_mean = column("t_mean")
+        V.tensor_tensor(t_mean[:], p_sigma_sum[:], inv_s[:], mult)
+        V.tensor_reduce(a1, by_run(p_sigma[:]), AXIS.X, add)
+
+        ka = sb.tile([P, 4, G], F32, name="ka")
+        r0 = column("r0")
+        r2 = column("r2")
+        r13 = sb.tile([P, 2], F32, name="r13")
+        V.scalar_tensor_tensor(ka[:, 0, :], a0, 1.0, k[:], mult, mult, accum_out=r0[:])
+        V.tensor_reduce(a2, by_run(p_c[:]), AXIS.X, add)
+        V.scalar_tensor_tensor(tan, a0, t_mean[:], a1, mult, sub)
+        inv_u = column("inv_u")
+        V.reciprocal(inv_u[:], r0[:])
+        V.scalar_tensor_tensor(ka[:, 2, :], a2, 1.0, k[:], mult, mult, accum_out=r2[:])
+        p_c_sigma = wide("p_c_sigma")
+        V.tensor_tensor(p_c_sigma[:], c[:], p_sigma[:], mult)
+        shift = sb.tile([P, 2, G], F32, name="shift")
+        V.scalar_tensor_tensor(shift[:], tan.unsqueeze(1).to_broadcast([P, 2, G]), nh[:], sums[:, 1:4:2, :], mult, mult)
+        c_mean = column("c_mean")
+        V.tensor_tensor(c_mean[:], r2[:], inv_u[:], mult)
+        V.tensor_reduce(a3, by_run(p_c_sigma[:]), AXIS.X, add)
+
+        shares = sb.tile([P, 2, G], F32, name="shares")
+        S.activation(shares[:], sums[:, 0:2, :], ACT.Copy, scale=inv_s[:])
+        phi = runs("phi")
+        S.activation(phi[:], tan, ACT.Copy, scale=nh[:])
+        out_factor = column("out_factor")
+        S.activation(out_factor[:], inv_u[:], ACT.Copy, scale=-OUT_SCALE)
+        p_out = wide("p_out")
+        S.activation(p_out[:], p[:], ACT.Copy, scale=out_factor[:])
+
+        f_t = wide("f_t")
+        V.tensor_tensor(f_t[:], ta_t[:], q1_t[:], mult)
+        f = bank("f", "bank1")
+        turn(f, f_t, range(BLOCKS))
+
+        yv = sb.tile([P, 2, G], F32, name="yv")
+        y0n, v = yv[:, 0, :], yv[:, 1, :]
+        V.scalar_tensor_tensor(y0n, ka[:, 0, :], c_mean[:], ka[:, 2, :], mult, sub)
+        moved = sb.tile([P, 2, G], F32, name="moved")
+        V.tensor_tensor(moved[:], sums[:, 2:5:2, :], shift[:], sub)
+        x1 = wide("x1")
+        V.scalar_tensor_tensor(by_run(x1[:]), by_run(c[:]), c_mean[:], spread(k[:]), sub, mult)
+        V.scalar_tensor_tensor(ka[:, 1, :], moved[:, 0, :], 1.0, k[:], mult, mult, accum_out=r13[:, 0:1])
+        V.scalar_tensor_tensor(ka[:, 3, :], moved[:, 1, :], 1.0, k[:], mult, mult, accum_out=r13[:, 1:2])
+        mn = column("mn")
+        mn_terms = runs("mn_terms")
+        V.scalar_tensor_tensor(mn_terms[:], y0n, nh[:], shares[:, 1, :], mult, mult, accum_out=mn[:])
+        zr = sb.tile([P, 2], F32, name="zr")
+        V.tensor_scalar(zr[:], r13[:], inv_u[:], None, mult)
+        y1n = runs("y1n")
+        V.scalar_tensor_tensor(y1n[:], ka[:, 1, :], c_mean[:], ka[:, 3, :], mult, sub)
+        x2 = wide("x2")
+        V.scalar_tensor_tensor(by_run(x2[:]), spread(y0n), nh[:], by_run(x1[:]), mult, sub)
+        z = zr[:, 0:1]
+        zt = column("zt")
+        V.tensor_tensor(zt[:], z, t_mean[:], add)
+        ntc = column("ntc")
+        V.scalar_tensor_tensor(ntc[:], c_mean[:], z, zr[:, 1:2], mult, sub)
+        x4 = wide("x4")
+        V.scalar_tensor_tensor(by_run(x4[:]), spread(phi[:]), z, by_run(x1[:]), add, mult)
+        v1 = runs("v1")
+        V.scalar_tensor_tensor(v1[:], y0n, zt[:], y1n[:], mult, sub)
+        ktc = runs("ktc")
+        S.activation(ktc[:], k[:], ACT.Copy, scale=ntc[:])
+        x3 = wide("x3")
+        V.scalar_tensor_tensor(x3[:, :half], x2[:, :half], mn[:], f[:, :half], sub, mult)
+        V.scalar_tensor_tensor(v, ka[:, 0, :], ntc[:], v1[:], mult, add)
+        V.scalar_tensor_tensor(x3[:, half:], x2[:, half:], mn[:], f[:, half:], sub, mult)
+        dd = runs("dd")
+        V.scalar_tensor_tensor(dd[:], v, nh[:], ktc[:], mult, add)
+        n_terms = sb.tile([P, 2, G], F32, name="n_terms")
+        n_sum = column("n_sum")
+        V.scalar_tensor_tensor(n_terms[:], yv[:], nh[:], shares[:], mult, mult, accum_out=n_sum[:])
+
+        halves = [slice(0, half), slice(half, SLOTS)]
+        run_halves = [slice(0, G // 2), slice(G // 2, G)]
+        x5, x6, x7 = wide("x5"), wide("x6"), wide("x7")
+        for cols, gs in zip(halves, run_halves):
+            V.scalar_tensor_tensor(
+                by_run(x5[:, cols]), by_run(x4[:, cols]), n_sum[:],
+                dd[:, gs].unsqueeze(2).to_broadcast([P, G // 2, RUN]), add, sub,
+            )
+        for cols in halves:
+            V.tensor_tensor(x6[:, cols], e[:, cols], x5[:, cols], mult)
+        for cols in halves:
+            V.tensor_tensor(x7[:, cols], x3[:, cols], x6[:, cols], add)
+        V.tensor_tensor(scattered[:].indirect(offsets[:]), x7[:], p_out[:], mult)
+
+        first = 0
+        for n, width in enumerate(STORE_WIDTHS):
+            cols = slice(first, first + width)
+            result = sb.tile([P, width], F32, name="result%d" % n)
+            V.tensor_tensor(result[:], scattered[:, cols], base_sb[:, cols], add)
+            queue = nc.sync if n % 2 == 0 else nc.scalar
+            queue.dma_start(out[:, cols], result[:])
+            first += width

@@ -62,9 +62,21 @@ def tile_attend_hvowncurve_crowdshy_s_kernel(
         offsets = sb.tile([P, SLOTS // 16], U16, name="offsets")
         nc.sync.dma_start(offsets[:], offs)
 
-        def load_scale_rows(name, scales):
-            window = sb.tile([P, T], U8, name=name)
-            V.memset(window[:].bitcast(I32), 0)
+        def clear_on_vector(words):
+            cut = words.shape[1] // 2 - 1
+            V.memset(words[:, :cut], 0)
+            V.memset(words[:, cut:], 0)
+
+        def clear_on_gpsimd(words):
+            nc.gpsimd.memset(words, 0)
+
+        def clear_shared(words, vector_share):
+            clear_on_vector(words[:, :vector_share])
+            clear_on_gpsimd(words[:, vector_share:])
+
+        def load_scale_rows(name, scales, tag, clear):
+            window = sb.tile([P, T], U8, name=name, tag=tag)
+            clear(window[:].bitcast(I32))
             for quad in range(4):
                 nc.sync.dma_start(
                     window[32 * quad : 32 * quad + 4, :].bitcast(I32),
@@ -77,9 +89,9 @@ def tile_attend_hvowncurve_crowdshy_s_kernel(
             nc.sync.dma_start(window[:].bitcast(I32), words[0].bitcast(I32))
             return window
 
-        def load_row(name, table, tag):
+        def load_row(name, table, tag, clear):
             window = sb.tile([P, T], F32, name=name, tag=tag)
-            V.memset(window[:], 0.0)
+            clear(window[:])
             nc.sync.dma_start(window[0:1, :], table[0:1, :])
             return window
 
@@ -90,11 +102,11 @@ def tile_attend_hvowncurve_crowdshy_s_kernel(
 
         def round_and_interleave(name, raw, tag):
             grouped = sb.tile([P, Q, PACK], BF16, name=name, tag=tag, align_bytes=64)
-            S.copy(grouped[:], raw[:].rearrange("p j w -> p w j"))
+            S.activation(grouped[:], raw[:].rearrange("p j w -> p w j"), ACT.Copy)
             return grouped
 
-        def quantise(name, grouped):
-            codes = sb.tile([P, Q], U32, name=name + "_codes", align_bytes=64)
+        def quantise(name, grouped, tag):
+            codes = sb.tile([P, Q], U32, name=name + "_codes", tag=tag, align_bytes=64)
             scales = sb.tile([P, Q], U8, name=name + "_scales", align_bytes=64)
             V.quantize_mx(out=codes[:].bitcast(FP8X4), scales=scales[:], in_=grouped[:].rearrange("p w j -> p (w j)"))
             return codes, scales
@@ -108,119 +120,113 @@ def tile_attend_hvowncurve_crowdshy_s_kernel(
             for j in blocks:
                 PE.transpose(target[:, block(j)], source[:, block(j)], identity[:])
 
-        key_scale_window = load_scale_rows("key_scale_window", keys_scales)
-        query_raw = load_rows("query_raw", query, "pool_buffer")
-        dquery_raw = load_rows("dquery_raw", dquery, "staging")
-        key_word_window = load_words("key_word_window", keys_words, "key_word_window")
-        cv1_window = load_row("cv1_window", cv1, "row_buffer")
-        cv2_window = load_row("cv2_window", cv2, "cv2_window")
-        val_scale_window = load_scale_rows("val_scale_window", vals_scales)
-
+        key_word_window = load_words("key_word_window", keys_words, "key_word_buffer")
+        query_raw = load_rows("query_raw", query, "query_staging")
+        key_scale_window = load_scale_rows("key_scale_window", keys_scales, "key_scale_buffer", clear_on_gpsimd)
+        cv2_window = load_row("cv2_window", cv2, "cv2_buffer", lambda w: clear_shared(w, 1280))
+        cv1_window = load_row("cv1_window", cv1, "cv1_buffer", lambda w: clear_shared(w, 1024))
+        val_scale_window = load_scale_rows("val_scale_window", vals_scales, "val_scale_window", clear_on_vector)
         identity = sb.tile([P, P], F32, name="identity")
         make_identity(nc, identity[:])
-        shyness = column("shyness")
-        nc.gpsimd.dma_start(shyness[:], shy)
 
         query_grouped = round_and_interleave("query_grouped", query_raw, "query_grouped")
-        dquery_grouped = round_and_interleave("dquery_grouped", dquery_raw, "dquery_grouped")
-        val_word_window = load_words("val_word_window", vals_words, "pool_buffer")
-        gout_raw = load_rows("gout_raw", gout, "staging")
+        val_word_window = load_words("val_word_window", vals_words, "query_staging")
 
-        key_scales = gather("key_scales", key_scale_window, U8, "key_scales")
         key_words = gather("key_words", key_word_window, U16, "key_words")
-        query_codes, query_scales = quantise("query", query_grouped)
+        dquery_raw = load_rows("dquery_raw", dquery, "key_word_buffer")
+        key_scales = gather("key_scales", key_scale_window, U8, "key_scales")
+        gout_raw = load_rows("gout_raw", gout, "key_scale_buffer")
 
-        cv1_picked = wide("cv1_picked")
-        S.activation(cv1_picked[:], cv1_window[:].indirect(offsets[:]), ACT.Copy)
-        cv1_turned = bank("cv1_turned", "bank0")
-        turn(cv1_turned, cv1_picked, range(BLOCKS))
+        cv2_picked = sb.tile([P, SLOTS], F32, name="cv2_picked", tag="cv2_picked", align_bytes=64)
+        S.activation(cv2_picked[:], cv2_window[:].indirect(offsets[:]), ACT.Copy)
+        shyness = sb.tile([P, 1], F32, name="shyness", tag="cv2_buffer")
+        nc.sync.dma_start(shyness[:], shy)
+        cv2_turned = bank("cv2_turned", "bank0")
+        turn(cv2_turned, cv2_picked, range(BLOCKS))
+        query_codes, query_scales = quantise("query", query_grouped, "cv2_picked")
         half = SLOTS // 2
-        cv2_turned = []
+        halves = [slice(0, half), slice(half, SLOTS)]
+        list_halves = [slice(0, half // 16), slice(half // 16, SLOTS // 16)]
+        run_halves = [slice(0, G // 2), slice(G // 2, G)]
+        cv1_turned = []
         for h in range(2):
-            picked = sb.tile([P, half], F32, name="cv2_picked%d" % h, tag="cv2_picked%d" % h, align_bytes=64)
-            S.activation(picked[:], cv2_window[:].indirect(offsets[:, h * half // 16 : (h + 1) * half // 16]), ACT.Copy)
-            turned = bank("cv2_turned%d" % h, "bank%d" % (1 + h))
+            picked = sb.tile([P, half], F32, name="cv1_picked%d" % h, tag="cv1_picked%d" % h, align_bytes=64)
+            S.activation(picked[:], cv1_window[:].indirect(offsets[:, list_halves[h]]), ACT.Copy)
+            turned = bank("cv1_turned%d" % h, "bank%d" % (1 + h))
             turn(turned, picked, range(BLOCKS // 2))
-            cv2_turned.append(turned)
-
-        base_sb = sb.tile([P, T], F32, name="base_sb", tag="row_buffer")
+            cv1_turned.append(turned)
+        base_sb = sb.tile([P, T], F32, name="base_sb", tag="cv1_buffer")
         nc.sync.dma_start(base_sb[:], base)
-        c1 = sb.tile([P, BLOCKS], F32, name="c1")
-        S.copy(c1[:], cv1_turned[:, 0:SLOTS:P])
 
-        def slot_major_product(name, tag, codes, scales):
+        a_t = bank("a_t", "bank3")
+        for j in range(BLOCKS):
+            PE.matmul_mx(
+                out=a_t[:, block(j)],
+                lhsT=key_words[:, block(j)].bitcast(FP4X4),
+                lhsT_scale=key_scales[:, block(j)],
+                rhs=query_codes[:].bitcast(FP8X4),
+                rhs_scale=query_scales[:],
+                start=True,
+                stop=True,
+            )
+        val_scales = gather("val_scales", val_scale_window, U8, "query_grouped")
+
+        def row_major_product(name, tag, codes, scales, words, word_scales):
             product = bank(name, tag)
-            for j in range(BLOCKS):
-                PE.matmul_mx(
-                    out=product[:, block(j)],
-                    lhsT=key_words[:, block(j)].bitcast(FP4X4),
-                    lhsT_scale=key_scales[:, block(j)],
-                    rhs=codes[:].bitcast(FP8X4),
-                    rhs_scale=scales[:],
-                    start=True,
-                    stop=True,
-                )
+            PE.matmul_mx(
+                out=product[:],
+                lhsT=codes[:].bitcast(FP8X4),
+                lhsT_scale=scales[:],
+                rhs=words[:].bitcast(FP4X4),
+                rhs_scale=word_scales[:],
+                start=True,
+                stop=True,
+            )
             return product
 
-        a_t = slot_major_product("a_t", "bank3", query_codes, query_scales)
-
-        c2 = sb.tile([P, BLOCKS], F32, name="c2")
-        u_t = sb.tile([P, SLOTS], F32, name="u_t", tag="u_buffer", align_bytes=64)
-        for h in range(2):
-            S.copy(c2[:, 2 * h : 2 * h + 2], cv2_turned[h][:, 0:half:P])
-            for j in (2 * h, 2 * h + 1):
-                S.activation(u_t[:, block(j)], a_t[:, block(j)], ACT.Identity, bias=c1[:, j : j + 1], scale=c2[:, j : j + 1])
-
-        dquery_codes, dquery_scales = quantise("dquery", dquery_grouped)
-        val_scales = gather("val_scales", val_scale_window, U8, "val_scales")
-        ta_t = slot_major_product("ta_t", "bank4", dquery_codes, dquery_scales)
-
-        s_t = wide("s_t")
-        V.tensor_tensor(s_t[:], a_t[:], u_t[:], mult)
+        u_t = wide("u_t")
         s = bank("s", "bank6")
-        turn(s, s_t, range(BLOCKS))
+        for h, cols in enumerate(halves):
+            for j in (2 * h, 2 * h + 1):
+                c2_j = cv2_turned[:, j * P : j * P + 1]
+                c1_j = cv1_turned[h][:, (j % 2) * P : (j % 2) * P + 1]
+                V.tensor_scalar(u_t[:, block(j)], a_t[:, block(j)], c2_j, c1_j, mult, add)
+        for h, cols in enumerate(halves):
+            s_t = sb.tile([P, half], F32, name="s_t%d" % h, tag="s_t%d" % h, align_bytes=64)
+            V.tensor_tensor(s_t[:], a_t[:, cols], u_t[:, cols], mult)
+            turn(s[:, cols], s_t, range(BLOCKS // 2))
 
+        dquery_grouped = round_and_interleave("dquery_grouped", dquery_raw, "cv1_picked0")
+        dquery_codes, dquery_scales = quantise("dquery", dquery_grouped, "dquery_codes")
+        ta = row_major_product("ta", "bank4", dquery_codes, dquery_scales, key_words, key_scales)
         minus_c1 = sb.tile([P, BLOCKS], F32, name="minus_c1")
-        S.activation(minus_c1[:], c1[:], ACT.Copy, scale=-1.0)
+        for h in range(2):
+            S.activation(minus_c1[:, 2 * h : 2 * h + 2], cv1_turned[h][:, 0:half:P], ACT.Copy, scale=-1.0)
         e_t = wide("e_t")
         for j in range(BLOCKS):
             S.activation(e_t[:, block(j)], u_t[:, block(j)], ACT.Identity, bias=minus_c1[:, j : j + 1], scale=2.0)
-        gout_grouped = round_and_interleave("gout_grouped", gout_raw, "cv2_picked1")
+        e = bank("e", "bank7")
+        turn(e, e_t, range(BLOCKS))
 
-        val_words = gather("val_words", val_word_window, U16, "u_buffer")
-        gout_codes, gout_scales = quantise("gout", gout_grouped)
-        c = bank("c", "bank5")
-        PE.matmul_mx(
-            out=c[:],
-            lhsT=gout_codes[:].bitcast(FP8X4),
-            lhsT_scale=gout_scales[:],
-            rhs=val_words[:].bitcast(FP4X4),
-            rhs_scale=val_scales[:],
-            start=True,
-            stop=True,
-        )
         minus_max = column("minus_max")
         V.tensor_reduce(minus_max[:], s[:], AXIS.X, ALU.max, negate=True)
         p = wide("p")
         p_sum = column("p_sum")
         S.activation(p[:], s[:], ACT.Exp, bias=minus_max[:], accum_out=p_sum[:])
 
-        scattered = sb.tile([P, T], F32, name="scattered", tag="pool_buffer")
+        val_words = gather("val_words", val_word_window, U16, "s_t0")
+        scattered = sb.tile([P, T], F32, name="scattered", tag="query_staging")
         nc.gpsimd.memset(scattered[:], 0.0)
-
-        sigma_t = wide("sigma_t")
-        V.tensor_tensor(sigma_t[:], ta_t[:], e_t[:], mult)
-        sigma = bank("sigma", "bank7")
-        turn(sigma, sigma_t, range(BLOCKS))
-
-        e = bank("e", "bank0")
-        turn(e, e_t, range(BLOCKS))
+        gout_grouped = round_and_interleave("gout_grouped", gout_raw, "cv1_picked1")
+        gout_codes, gout_scales = quantise("gout", gout_grouped, "gout_codes")
+        c = row_major_product("c", "bank5", gout_codes, gout_scales, val_words, val_scales)
 
         minus_shy = column("minus_shy")
         S.activation(minus_shy[:], shyness[:], ACT.Copy, scale=-1.0)
 
         sums = sb.tile([P, 5, G], F32, name="sums")
         tan, a0, a1, a2, a3 = [sums[:, n, :] for n in range(5)]
+
         inv_s = column("inv_s")
         V.reciprocal(inv_s[:], p_sum[:])
         V.tensor_reduce(a0, by_run(p[:]), AXIS.X, add)
@@ -229,107 +235,94 @@ def tile_attend_hvowncurve_crowdshy_s_kernel(
         k = runs("k")
         S.activation(k[:], a0, ACT.Exp, scale=nh[:])
 
+        two_c2 = sb.tile([P, BLOCKS], F32, name="two_c2")
+        S.activation(two_c2[:], cv2_turned[:, 0:SLOTS:P], ACT.Copy, scale=2.0)
         e_sq = wide("e_sq")
         S.activation(e_sq[:], e_t[:], ACT.Square)
-        two_c2 = sb.tile([P, BLOCKS], F32, name="two_c2")
-        S.activation(two_c2[:], c2[:], ACT.Copy, scale=2.0)
         q1_t = wide("q1_t")
         for j in range(BLOCKS):
             S.activation(q1_t[:, block(j)], e_sq[:, block(j)], ACT.Identity, bias=two_c2[:, j : j + 1])
+        q1 = bank("q1", "bank1")
+        turn(q1, q1_t, range(BLOCKS))
 
-        p_sigma = wide("p_sigma")
-        p_sigma_sum = column("p_sigma_sum")
-        V.scalar_tensor_tensor(p_sigma[:], sigma[:], 1.0, p[:], mult, mult, accum_out=p_sigma_sum[:])
-        p_c = wide("p_c")
+        p_e, p_sigma, p_c, p_c_sigma, p_q1, p_f = [wide(n) for n in ("p_e", "p_sigma", "p_c", "p_c_sigma", "p_q1", "p_f")]
+        p_sigma_sum, t_mean, r0, r2, inv_u, c_mean = [column(n) for n in ("p_sigma_sum", "t_mean", "r0", "r2", "inv_u", "c_mean")]
+        ka = sb.tile([P, 4, G], F32, name="ka")
+        r13 = sb.tile([P, 2], F32, name="r13")
+        shift = sb.tile([P, 2, G], F32, name="shift")
+        V.tensor_tensor(p_e[:], e[:], p[:], mult)
+        V.scalar_tensor_tensor(p_sigma[:], ta[:], 1.0, p_e[:], mult, mult, accum_out=p_sigma_sum[:])
         V.tensor_tensor(p_c[:], c[:], p[:], mult)
-        t_mean = column("t_mean")
         V.tensor_tensor(t_mean[:], p_sigma_sum[:], inv_s[:], mult)
         V.tensor_reduce(a1, by_run(p_sigma[:]), AXIS.X, add)
-
-        ka = sb.tile([P, 4, G], F32, name="ka")
-        r0 = column("r0")
-        r2 = column("r2")
-        r13 = sb.tile([P, 2], F32, name="r13")
         V.scalar_tensor_tensor(ka[:, 0, :], a0, 1.0, k[:], mult, mult, accum_out=r0[:])
         V.tensor_reduce(a2, by_run(p_c[:]), AXIS.X, add)
         V.scalar_tensor_tensor(tan, a0, t_mean[:], a1, mult, sub)
-        inv_u = column("inv_u")
         V.reciprocal(inv_u[:], r0[:])
-        V.scalar_tensor_tensor(ka[:, 2, :], a2, 1.0, k[:], mult, mult, accum_out=r2[:])
-        p_c_sigma = wide("p_c_sigma")
-        V.tensor_tensor(p_c_sigma[:], c[:], p_sigma[:], mult)
-        shift = sb.tile([P, 2, G], F32, name="shift")
-        V.scalar_tensor_tensor(shift[:], tan.unsqueeze(1).to_broadcast([P, 2, G]), nh[:], sums[:, 1:4:2, :], mult, mult)
-        c_mean = column("c_mean")
-        V.tensor_tensor(c_mean[:], r2[:], inv_u[:], mult)
-        V.tensor_reduce(a3, by_run(p_c_sigma[:]), AXIS.X, add)
-
         shares = sb.tile([P, 2, G], F32, name="shares")
         S.activation(shares[:], sums[:, 0:2, :], ACT.Copy, scale=inv_s[:])
         phi = runs("phi")
         S.activation(phi[:], tan, ACT.Copy, scale=nh[:])
-        out_factor = column("out_factor")
+        V.scalar_tensor_tensor(ka[:, 2, :], a2, 1.0, k[:], mult, mult, accum_out=r2[:])
+        out_factor, nhf = column("out_factor"), column("nhf")
         S.activation(out_factor[:], inv_u[:], ACT.Copy, scale=-OUT_SCALE)
-        p_out = wide("p_out")
-        S.activation(p_out[:], p[:], ACT.Copy, scale=out_factor[:])
-
-        f_t = wide("f_t")
-        V.tensor_tensor(f_t[:], ta_t[:], q1_t[:], mult)
-        f = bank("f", "bank1")
-        turn(f, f_t, range(BLOCKS))
-
+        kf = runs("kf")
+        S.activation(kf[:], k[:], ACT.Copy, scale=out_factor[:])
+        S.activation(nhf[:], nh[:], ACT.Copy, scale=out_factor[:])
+        V.tensor_tensor(p_c_sigma[:], c[:], p_sigma[:], mult)
+        V.scalar_tensor_tensor(shift[:], tan.unsqueeze(1).to_broadcast([P, 2, G]), nh[:], sums[:, 1:4:2, :], mult, mult)
+        V.tensor_tensor(c_mean[:], r2[:], inv_u[:], mult)
+        V.tensor_reduce(a3, by_run(p_c_sigma[:]), AXIS.X, add)
         yv = sb.tile([P, 2, G], F32, name="yv")
         y0n, v = yv[:, 0, :], yv[:, 1, :]
         V.scalar_tensor_tensor(y0n, ka[:, 0, :], c_mean[:], ka[:, 2, :], mult, sub)
+        V.tensor_tensor(p_q1[:], q1[:], p[:], mult)
         moved = sb.tile([P, 2, G], F32, name="moved")
         V.tensor_tensor(moved[:], sums[:, 2:5:2, :], shift[:], sub)
         x1 = wide("x1")
-        V.scalar_tensor_tensor(by_run(x1[:]), by_run(c[:]), c_mean[:], spread(k[:]), sub, mult)
+        V.scalar_tensor_tensor(by_run(x1[:]), by_run(c[:]), c_mean[:], spread(kf[:]), sub, mult)
         V.scalar_tensor_tensor(ka[:, 1, :], moved[:, 0, :], 1.0, k[:], mult, mult, accum_out=r13[:, 0:1])
         V.scalar_tensor_tensor(ka[:, 3, :], moved[:, 1, :], 1.0, k[:], mult, mult, accum_out=r13[:, 1:2])
         mn = column("mn")
         mn_terms = runs("mn_terms")
-        V.scalar_tensor_tensor(mn_terms[:], y0n, nh[:], shares[:, 1, :], mult, mult, accum_out=mn[:])
+        V.scalar_tensor_tensor(mn_terms[:], y0n, nhf[:], shares[:, 1, :], mult, mult, accum_out=mn[:])
         zr = sb.tile([P, 2], F32, name="zr")
         V.tensor_scalar(zr[:], r13[:], inv_u[:], None, mult)
+        z = zr[:, 0:1]
+        V.tensor_tensor(p_f[:], ta[:], p_q1[:], mult)
         y1n = runs("y1n")
         V.scalar_tensor_tensor(y1n[:], ka[:, 1, :], c_mean[:], ka[:, 3, :], mult, sub)
-        x2 = wide("x2")
-        V.scalar_tensor_tensor(by_run(x2[:]), spread(y0n), nh[:], by_run(x1[:]), mult, sub)
-        z = zr[:, 0:1]
         zt = column("zt")
         V.tensor_tensor(zt[:], z, t_mean[:], add)
         ntc = column("ntc")
         V.scalar_tensor_tensor(ntc[:], c_mean[:], z, zr[:, 1:2], mult, sub)
-        x4 = wide("x4")
-        V.scalar_tensor_tensor(by_run(x4[:]), spread(phi[:]), z, by_run(x1[:]), add, mult)
+        ktc = runs("ktc")
+        S.activation(ktc[:], kf[:], ACT.Copy, scale=ntc[:])
+        x2 = wide("x2")
+        V.scalar_tensor_tensor(by_run(x2[:]), spread(y0n), nhf[:], by_run(x1[:]), mult, sub)
         v1 = runs("v1")
         V.scalar_tensor_tensor(v1[:], y0n, zt[:], y1n[:], mult, sub)
-        ktc = runs("ktc")
-        S.activation(ktc[:], k[:], ACT.Copy, scale=ntc[:])
-        x3 = wide("x3")
-        V.scalar_tensor_tensor(x3[:, :half], x2[:, :half], mn[:], f[:, :half], sub, mult)
+        x4 = wide("x4")
+        V.scalar_tensor_tensor(by_run(x4[:]), spread(phi[:]), z, by_run(x1[:]), add, mult)
         V.scalar_tensor_tensor(v, ka[:, 0, :], ntc[:], v1[:], mult, add)
-        V.scalar_tensor_tensor(x3[:, half:], x2[:, half:], mn[:], f[:, half:], sub, mult)
-        dd = runs("dd")
-        V.scalar_tensor_tensor(dd[:], v, nh[:], ktc[:], mult, add)
+        x3 = wide("x3")
+        V.scalar_tensor_tensor(x3[:, :half], x2[:, :half], mn[:], p_f[:, :half], sub, mult)
         n_terms = sb.tile([P, 2, G], F32, name="n_terms")
         n_sum = column("n_sum")
-        V.scalar_tensor_tensor(n_terms[:], yv[:], nh[:], shares[:], mult, mult, accum_out=n_sum[:])
+        V.scalar_tensor_tensor(n_terms[:], yv[:], nhf[:], shares[:], mult, mult, accum_out=n_sum[:])
+        dd = runs("dd")
+        V.scalar_tensor_tensor(dd[:], v, nhf[:], ktc[:], mult, add)
+        V.scalar_tensor_tensor(x3[:, half:], x2[:, half:], mn[:], p_f[:, half:], sub, mult)
 
-        halves = [slice(0, half), slice(half, SLOTS)]
-        run_halves = [slice(0, G // 2), slice(G // 2, G)]
-        x5, x6, x7 = wide("x5"), wide("x6"), wide("x7")
+        x5, x6 = wide("x5"), wide("x6")
         for cols, gs in zip(halves, run_halves):
             V.scalar_tensor_tensor(
                 by_run(x5[:, cols]), by_run(x4[:, cols]), n_sum[:],
                 dd[:, gs].unsqueeze(2).to_broadcast([P, G // 2, RUN]), add, sub,
             )
         for cols in halves:
-            V.tensor_tensor(x6[:, cols], e[:, cols], x5[:, cols], mult)
-        for cols in halves:
-            V.tensor_tensor(x7[:, cols], x3[:, cols], x6[:, cols], add)
-        V.tensor_tensor(scattered[:].indirect(offsets[:]), x7[:], p_out[:], mult)
+            V.tensor_tensor(x6[:, cols], p_e[:, cols], x5[:, cols], mult)
+        V.tensor_tensor(scattered[:].indirect(offsets[:]), x3[:], x6[:], add)
 
         first = 0
         for n, width in enumerate(STORE_WIDTHS):

@@ -22,6 +22,7 @@ G = SLOTS // RUN
 BLOCKS = SLOTS // P
 PACK = 4
 OUT_SCALE = 512.0
+CV1_ROW, CV2_ROW = 80, 16
 STORE_WIDTHS = (256, 512, 512, 512, 256)
 
 FLOPS = 3 * 2 * D * Q * SLOTS
@@ -53,9 +54,6 @@ def tile_attend_hvowncurve_crowdshy_s_kernel(
         def by_run(ap):
             return ap.rearrange("p (g j) -> p g j", j=RUN)
 
-        def spread(ap):
-            return ap.unsqueeze(2).to_broadcast([P, G, RUN])
-
         def block(j):
             return slice(j * P, (j + 1) * P)
 
@@ -84,20 +82,20 @@ def tile_attend_hvowncurve_crowdshy_s_kernel(
                 )
             return window
 
-        def load_words(name, words, tag):
+        def load_words(name, words, tag, queue):
             window = sb.tile([P, T], U16, name=name, tag=tag)
-            nc.sync.dma_start(window[:].bitcast(I32), words[0].bitcast(I32))
+            queue.dma_start(window[:].bitcast(I32), words[0].bitcast(I32))
             return window
 
-        def load_row(name, table, tag, clear):
+        def load_row(name, table, row, tag, clear, queue):
             window = sb.tile([P, T], F32, name=name, tag=tag)
             clear(window[:])
-            nc.sync.dma_start(window[0:1, :], table[0:1, :])
+            queue.dma_start(window[row : row + 1, :], table[row : row + 1, :])
             return window
 
-        def load_rows(name, rows, tag):
+        def load_rows(name, rows, tag, queue):
             raw = sb.tile([P, PACK, Q], F32, name=name, tag=tag)
-            nc.sync.dma_start(raw[:], rows.rearrange("(p j) w -> p j w", j=PACK))
+            queue.dma_start(raw[:], rows.rearrange("(p j) w -> p j w", j=PACK))
             return raw
 
         def round_and_interleave(name, raw, tag):
@@ -120,30 +118,30 @@ def tile_attend_hvowncurve_crowdshy_s_kernel(
             for j in blocks:
                 PE.transpose(target[:, block(j)], source[:, block(j)], identity[:])
 
-        key_word_window = load_words("key_word_window", keys_words, "key_word_buffer")
-        query_raw = load_rows("query_raw", query, "query_staging")
+        query_raw = load_rows("query_raw", query, "query_staging", nc.sync)
+        key_word_window = load_words("key_word_window", keys_words, "key_word_buffer", nc.sync)
         key_scale_window = load_scale_rows("key_scale_window", keys_scales, "key_scale_buffer", clear_on_gpsimd)
-        cv2_window = load_row("cv2_window", cv2, "cv2_buffer", lambda w: clear_shared(w, 1280))
-        cv1_window = load_row("cv1_window", cv1, "cv1_buffer", lambda w: clear_shared(w, 1024))
+        cv2_window = load_row("cv2_window", cv2, CV2_ROW, "cv2_buffer", lambda w: clear_shared(w, 1280), nc.scalar)
+        cv1_window = load_row("cv1_window", cv1, CV1_ROW, "cv1_buffer", lambda w: clear_shared(w, 1024), nc.sync)
         val_scale_window = load_scale_rows("val_scale_window", vals_scales, "val_scale_window", clear_on_vector)
         identity = sb.tile([P, P], F32, name="identity")
         make_identity(nc, identity[:])
 
         query_grouped = round_and_interleave("query_grouped", query_raw, "query_grouped")
-        val_word_window = load_words("val_word_window", vals_words, "query_staging")
+        val_word_window = load_words("val_word_window", vals_words, "query_staging", nc.scalar)
 
         key_words = gather("key_words", key_word_window, U16, "key_words")
-        dquery_raw = load_rows("dquery_raw", dquery, "key_word_buffer")
+        shyness = sb.tile([P, 1], F32, name="shyness", tag="key_word_buffer")
+        nc.sync.dma_start(shyness[:], shy)
         key_scales = gather("key_scales", key_scale_window, U8, "key_scales")
-        gout_raw = load_rows("gout_raw", gout, "key_scale_buffer")
+        gout_raw = load_rows("gout_raw", gout, "key_scale_buffer", nc.sync)
 
         cv2_picked = sb.tile([P, SLOTS], F32, name="cv2_picked", tag="cv2_picked", align_bytes=64)
         S.activation(cv2_picked[:], cv2_window[:].indirect(offsets[:]), ACT.Copy)
-        shyness = sb.tile([P, 1], F32, name="shyness", tag="cv2_buffer")
-        nc.sync.dma_start(shyness[:], shy)
+        dquery_raw = load_rows("dquery_raw", dquery, "cv2_buffer", nc.scalar)
         cv2_turned = bank("cv2_turned", "bank0")
         turn(cv2_turned, cv2_picked, range(BLOCKS))
-        query_codes, query_scales = quantise("query", query_grouped, "cv2_picked")
+        query_codes, query_scales = quantise("query", query_grouped, "query_codes")
         half = SLOTS // 2
         halves = [slice(0, half), slice(half, SLOTS)]
         list_halves = [slice(0, half // 16), slice(half // 16, SLOTS // 16)]
@@ -171,25 +169,23 @@ def tile_attend_hvowncurve_crowdshy_s_kernel(
             )
         val_scales = gather("val_scales", val_scale_window, U8, "query_grouped")
 
-        def row_major_product(name, tag, codes, scales, words, word_scales):
-            product = bank(name, tag)
+        def row_major_product(product, codes, scales, words, word_scales):
             PE.matmul_mx(
-                out=product[:],
+                out=product,
                 lhsT=codes[:].bitcast(FP8X4),
                 lhsT_scale=scales[:],
-                rhs=words[:].bitcast(FP4X4),
-                rhs_scale=word_scales[:],
+                rhs=words.bitcast(FP4X4),
+                rhs_scale=word_scales,
                 start=True,
                 stop=True,
             )
-            return product
 
         u_t = wide("u_t")
         s = bank("s", "bank6")
         for h, cols in enumerate(halves):
             for j in (2 * h, 2 * h + 1):
-                c2_j = cv2_turned[:, j * P : j * P + 1]
-                c1_j = cv1_turned[h][:, (j % 2) * P : (j % 2) * P + 1]
+                c2_j = cv2_turned[:, j * P + CV2_ROW : j * P + CV2_ROW + 1]
+                c1_j = cv1_turned[h][:, (j % 2) * P + CV1_ROW : (j % 2) * P + CV1_ROW + 1]
                 V.tensor_scalar(u_t[:, block(j)], a_t[:, block(j)], c2_j, c1_j, mult, add)
         for h, cols in enumerate(halves):
             s_t = sb.tile([P, half], F32, name="s_t%d" % h, tag="s_t%d" % h, align_bytes=64)
@@ -198,28 +194,33 @@ def tile_attend_hvowncurve_crowdshy_s_kernel(
 
         dquery_grouped = round_and_interleave("dquery_grouped", dquery_raw, "cv1_picked0")
         dquery_codes, dquery_scales = quantise("dquery", dquery_grouped, "dquery_codes")
-        ta = row_major_product("ta", "bank4", dquery_codes, dquery_scales, key_words, key_scales)
+        ta = bank("ta", "bank4")
+        row_major_product(ta[:], dquery_codes, dquery_scales, key_words[:], key_scales[:])
         minus_c1 = sb.tile([P, BLOCKS], F32, name="minus_c1")
         for h in range(2):
-            S.activation(minus_c1[:, 2 * h : 2 * h + 2], cv1_turned[h][:, 0:half:P], ACT.Copy, scale=-1.0)
+            S.activation(minus_c1[:, 2 * h : 2 * h + 2], cv1_turned[h][:, CV1_ROW:half:P], ACT.Copy, scale=-1.0)
         e_t = wide("e_t")
         for j in range(BLOCKS):
             S.activation(e_t[:, block(j)], u_t[:, block(j)], ACT.Identity, bias=minus_c1[:, j : j + 1], scale=2.0)
         e = bank("e", "bank7")
         turn(e, e_t, range(BLOCKS))
 
+        val_words = []
+        for h in range(2):
+            val_words.append(sb.tile([P, half], U16, name="val_words%d" % h, tag="s_t%d" % h, align_bytes=64))
+        V.tensor_copy(val_words[0][:], val_word_window[:].indirect(offsets[:, list_halves[0]]))
         minus_max = column("minus_max")
         V.tensor_reduce(minus_max[:], s[:], AXIS.X, ALU.max, negate=True)
         p = wide("p")
         p_sum = column("p_sum")
         S.activation(p[:], s[:], ACT.Exp, bias=minus_max[:], accum_out=p_sum[:])
 
-        val_words = gather("val_words", val_word_window, U16, "s_t0")
-        scattered = sb.tile([P, T], F32, name="scattered", tag="query_staging")
-        nc.gpsimd.memset(scattered[:], 0.0)
+        V.tensor_copy(val_words[1][:], val_word_window[:].indirect(offsets[:, list_halves[1]]))
         gout_grouped = round_and_interleave("gout_grouped", gout_raw, "cv1_picked1")
         gout_codes, gout_scales = quantise("gout", gout_grouped, "gout_codes")
-        c = row_major_product("c", "bank5", gout_codes, gout_scales, val_words, val_scales)
+        c = bank("c", "bank5")
+        for h, cols in enumerate(halves):
+            row_major_product(c[:, cols], gout_codes, gout_scales, val_words[h][:], val_scales[:, cols])
 
         minus_shy = column("minus_shy")
         S.activation(minus_shy[:], shyness[:], ACT.Copy, scale=-1.0)
@@ -227,16 +228,25 @@ def tile_attend_hvowncurve_crowdshy_s_kernel(
         sums = sb.tile([P, 5, G], F32, name="sums")
         tan, a0, a1, a2, a3 = [sums[:, n, :] for n in range(5)]
 
+        def run_sums_on_gpsimd(name, target, source):
+            fours = sb.tile([P, G, 4], F32, name=name + "_fours")
+            twos = sb.tile([P, G, 2], F32, name=name + "_twos", tag=name + "_twos")
+            nc.gpsimd.tensor_tensor(fours[:], by_run(source)[:, :, 0:4], by_run(source)[:, :, 4:8], add)
+            nc.gpsimd.tensor_tensor(twos[:], fours[:, :, 0:2], fours[:, :, 2:4], add)
+            nc.gpsimd.tensor_tensor(target, twos[:, :, 0], twos[:, :, 1], add)
+
         inv_s = column("inv_s")
+        p_e = wide("p_e")
+        V.tensor_tensor(p_e[:], e[:], p[:], mult)
         V.reciprocal(inv_s[:], p_sum[:])
-        V.tensor_reduce(a0, by_run(p[:]), AXIS.X, add)
+        run_sums_on_gpsimd("p", a0, p[:])
         nh = column("nh")
         S.activation(nh[:], inv_s[:], ACT.Copy, scale=minus_shy[:])
         k = runs("k")
         S.activation(k[:], a0, ACT.Exp, scale=nh[:])
 
         two_c2 = sb.tile([P, BLOCKS], F32, name="two_c2")
-        S.activation(two_c2[:], cv2_turned[:, 0:SLOTS:P], ACT.Copy, scale=2.0)
+        S.activation(two_c2[:], cv2_turned[:, CV2_ROW:SLOTS:P], ACT.Copy, scale=2.0)
         e_sq = wide("e_sq")
         S.activation(e_sq[:], e_t[:], ACT.Square)
         q1_t = wide("q1_t")
@@ -245,51 +255,48 @@ def tile_attend_hvowncurve_crowdshy_s_kernel(
         q1 = bank("q1", "bank1")
         turn(q1, q1_t, range(BLOCKS))
 
-        p_e, p_sigma, p_c, p_c_sigma, p_q1, p_f = [wide(n) for n in ("p_e", "p_sigma", "p_c", "p_c_sigma", "p_q1", "p_f")]
+        p_sigma, p_c, p_c_sigma, p_q1, p_f = [wide(n) for n in ("p_sigma", "p_c", "p_c_sigma", "p_q1", "p_f")]
         p_sigma_sum, t_mean, r0, r2, inv_u, c_mean = [column(n) for n in ("p_sigma_sum", "t_mean", "r0", "r2", "inv_u", "c_mean")]
         ka = sb.tile([P, 4, G], F32, name="ka")
         r13 = sb.tile([P, 2], F32, name="r13")
         shift = sb.tile([P, 2, G], F32, name="shift")
-        V.tensor_tensor(p_e[:], e[:], p[:], mult)
         V.scalar_tensor_tensor(p_sigma[:], ta[:], 1.0, p_e[:], mult, mult, accum_out=p_sigma_sum[:])
         V.tensor_tensor(p_c[:], c[:], p[:], mult)
-        V.tensor_tensor(t_mean[:], p_sigma_sum[:], inv_s[:], mult)
+        run_sums_on_gpsimd("p_c", a2, p_c[:])
+        scattered = sb.tile([P, T], F32, name="scattered", tag="p_c_twos")
+        nc.gpsimd.memset(scattered[:], 0.0)
+        S.activation(t_mean[:], p_sigma_sum[:], ACT.Copy, scale=inv_s[:])
+        V.tensor_tensor(p_c_sigma[:], c[:], p_sigma[:], mult)
         V.tensor_reduce(a1, by_run(p_sigma[:]), AXIS.X, add)
+        V.tensor_reduce(a3, by_run(p_c_sigma[:]), AXIS.X, add)
         V.scalar_tensor_tensor(ka[:, 0, :], a0, 1.0, k[:], mult, mult, accum_out=r0[:])
-        V.tensor_reduce(a2, by_run(p_c[:]), AXIS.X, add)
         V.scalar_tensor_tensor(tan, a0, t_mean[:], a1, mult, sub)
+        V.scalar_tensor_tensor(ka[:, 2, :], a2, 1.0, k[:], mult, mult, accum_out=r2[:])
         V.reciprocal(inv_u[:], r0[:])
         shares = sb.tile([P, 2, G], F32, name="shares")
         S.activation(shares[:], sums[:, 0:2, :], ACT.Copy, scale=inv_s[:])
         phi = runs("phi")
         S.activation(phi[:], tan, ACT.Copy, scale=nh[:])
-        V.scalar_tensor_tensor(ka[:, 2, :], a2, 1.0, k[:], mult, mult, accum_out=r2[:])
+        V.scalar_tensor_tensor(shift[:], tan.unsqueeze(1).to_broadcast([P, 2, G]), nh[:], sums[:, 1:4:2, :], mult, mult)
         out_factor, nhf = column("out_factor"), column("nhf")
         S.activation(out_factor[:], inv_u[:], ACT.Copy, scale=-OUT_SCALE)
         kf = runs("kf")
         S.activation(kf[:], k[:], ACT.Copy, scale=out_factor[:])
         S.activation(nhf[:], nh[:], ACT.Copy, scale=out_factor[:])
-        V.tensor_tensor(p_c_sigma[:], c[:], p_sigma[:], mult)
-        V.scalar_tensor_tensor(shift[:], tan.unsqueeze(1).to_broadcast([P, 2, G]), nh[:], sums[:, 1:4:2, :], mult, mult)
         V.tensor_tensor(c_mean[:], r2[:], inv_u[:], mult)
-        V.tensor_reduce(a3, by_run(p_c_sigma[:]), AXIS.X, add)
+        moved = sb.tile([P, 2, G], F32, name="moved")
+        V.tensor_tensor(moved[:], sums[:, 2:5:2, :], shift[:], sub)
         yv = sb.tile([P, 2, G], F32, name="yv")
         y0n, v = yv[:, 0, :], yv[:, 1, :]
         V.scalar_tensor_tensor(y0n, ka[:, 0, :], c_mean[:], ka[:, 2, :], mult, sub)
-        V.tensor_tensor(p_q1[:], q1[:], p[:], mult)
-        moved = sb.tile([P, 2, G], F32, name="moved")
-        V.tensor_tensor(moved[:], sums[:, 2:5:2, :], shift[:], sub)
-        x1 = wide("x1")
-        V.scalar_tensor_tensor(by_run(x1[:]), by_run(c[:]), c_mean[:], spread(kf[:]), sub, mult)
         V.scalar_tensor_tensor(ka[:, 1, :], moved[:, 0, :], 1.0, k[:], mult, mult, accum_out=r13[:, 0:1])
         V.scalar_tensor_tensor(ka[:, 3, :], moved[:, 1, :], 1.0, k[:], mult, mult, accum_out=r13[:, 1:2])
         mn = column("mn")
         mn_terms = runs("mn_terms")
         V.scalar_tensor_tensor(mn_terms[:], y0n, nhf[:], shares[:, 1, :], mult, mult, accum_out=mn[:])
         zr = sb.tile([P, 2], F32, name="zr")
-        V.tensor_scalar(zr[:], r13[:], inv_u[:], None, mult)
+        V.tensor_tensor(zr[:], r13[:], inv_u[:].to_broadcast([P, 2]), mult)
         z = zr[:, 0:1]
-        V.tensor_tensor(p_f[:], ta[:], p_q1[:], mult)
         y1n = runs("y1n")
         V.scalar_tensor_tensor(y1n[:], ka[:, 1, :], c_mean[:], ka[:, 3, :], mult, sub)
         zt = column("zt")
@@ -298,27 +305,35 @@ def tile_attend_hvowncurve_crowdshy_s_kernel(
         V.scalar_tensor_tensor(ntc[:], c_mean[:], z, zr[:, 1:2], mult, sub)
         ktc = runs("ktc")
         S.activation(ktc[:], kf[:], ACT.Copy, scale=ntc[:])
-        x2 = wide("x2")
-        V.scalar_tensor_tensor(by_run(x2[:]), spread(y0n), nhf[:], by_run(x1[:]), mult, sub)
         v1 = runs("v1")
         V.scalar_tensor_tensor(v1[:], y0n, zt[:], y1n[:], mult, sub)
-        x4 = wide("x4")
-        V.scalar_tensor_tensor(by_run(x4[:]), spread(phi[:]), z, by_run(x1[:]), add, mult)
         V.scalar_tensor_tensor(v, ka[:, 0, :], ntc[:], v1[:], mult, add)
-        x3 = wide("x3")
-        V.scalar_tensor_tensor(x3[:, :half], x2[:, :half], mn[:], p_f[:, :half], sub, mult)
         n_terms = sb.tile([P, 2, G], F32, name="n_terms")
         n_sum = column("n_sum")
         V.scalar_tensor_tensor(n_terms[:], yv[:], nhf[:], shares[:], mult, mult, accum_out=n_sum[:])
         dd = runs("dd")
         V.scalar_tensor_tensor(dd[:], v, nhf[:], ktc[:], mult, add)
-        V.scalar_tensor_tensor(x3[:, half:], x2[:, half:], mn[:], p_f[:, half:], sub, mult)
 
-        x5, x6 = wide("x5"), wide("x6")
+        x1, x2, x3, x4, x5, x6 = [wide("x%d" % n) for n in range(1, 7)]
+
+        def spread_half(ap, gs):
+            return ap[:, gs].unsqueeze(2).to_broadcast([P, G // 2, RUN])
+
+        for cols in halves:
+            V.tensor_tensor(p_q1[:, cols], q1[:, cols], p[:, cols], mult)
+        for cols in halves:
+            V.tensor_tensor(p_f[:, cols], ta[:, cols], p_q1[:, cols], mult)
+        for cols, gs in zip(halves, run_halves):
+            V.scalar_tensor_tensor(by_run(x1[:, cols]), by_run(c[:, cols]), c_mean[:], spread_half(kf, gs), sub, mult)
+        for cols, gs in zip(halves, run_halves):
+            V.scalar_tensor_tensor(by_run(x2[:, cols]), spread_half(y0n, gs), nhf[:], by_run(x1[:, cols]), mult, sub)
+        for cols, gs in zip(halves, run_halves):
+            V.scalar_tensor_tensor(by_run(x4[:, cols]), spread_half(phi, gs), z, by_run(x1[:, cols]), add, mult)
+        for cols in halves:
+            V.scalar_tensor_tensor(x3[:, cols], x2[:, cols], mn[:], p_f[:, cols], sub, mult)
         for cols, gs in zip(halves, run_halves):
             V.scalar_tensor_tensor(
-                by_run(x5[:, cols]), by_run(x4[:, cols]), n_sum[:],
-                dd[:, gs].unsqueeze(2).to_broadcast([P, G // 2, RUN]), add, sub,
+                by_run(x5[:, cols]), by_run(x4[:, cols]), n_sum[:], spread_half(dd, gs), add, sub
             )
         for cols in halves:
             V.tensor_tensor(x6[:, cols], p_e[:, cols], x5[:, cols], mult)

from contextlib import ExitStack

import concourse.mybir as mybir
from concourse.masks import make_identity

F32 = mybir.dt.float32
BF16 = mybir.dt.bfloat16
I32 = mybir.dt.int32
U32 = mybir.dt.uint32
U16 = mybir.dt.uint16
U8 = mybir.dt.uint8
FP8X4 = mybir.dt.float8_e4m3fn_x4
FP4X4 = mybir.dt.float4_e2m1fn_x4
ALU = mybir.AluOpType
ACT = mybir.ActivationFunctionType
AXIS = mybir.AxisListType

P = 128
D, T, SLOTS, Q = 512, 2048, 512, 128
RUN = 8
G = SLOTS // RUN
BLOCKS = SLOTS // P
PACK = 4
OUT_SCALE = 512.0
CV1_ROW, CV2_ROW = 80, 16
STORE_WIDTHS = (256, 512, 512, 512, 256)

FLOPS = 3 * 2 * D * Q * SLOTS


def tile_attend_hvowncurve_crowdshy_s_kernel(
    tc, query, keys_words, keys_scales, cv1, cv2, shy, gout, vals_words, vals_scales, dquery, base, offs, out
):
    nc = tc.nc
    V, S, PE = nc.vector, nc.scalar, nc.tensor
    mult, add, sub = ALU.mult, ALU.add, ALU.subtract

    with ExitStack() as ctx:
        sb = ctx.enter_context(tc.tile_pool(name="sb", bufs=1))
        ps = ctx.enter_context(tc.psum_pool(name="ps", bufs=1))

        def wide(name):
            return sb.tile([P, SLOTS], F32, name=name)

        def runs(name):
            return sb.tile([P, G], F32, name=name)

        def column(name):
            return sb.tile([P, 1], F32, name=name)

        def bank(name, tag):
            return ps.tile([P, SLOTS], F32, name=name, tag=tag)

        def by_run(ap):
            return ap.rearrange("p (g j) -> p g j", j=RUN)

        def block(j):
            return slice(j * P, (j + 1) * P)

        offsets = sb.tile([P, SLOTS // 16], U16, name="offsets")
        nc.sync.dma_start(offsets[:], offs)

        def clear_on_vector(words):
            cut = words.shape[1] // 2 - 1
            V.memset(words[:, :cut], 0)
            V.memset(words[:, cut:], 0)

        def clear_on_gpsimd(words):
            nc.gpsimd.memset(words, 0)

        def clear_shared(words, vector_share):
            clear_on_vector(words[:, :vector_share])
            clear_on_gpsimd(words[:, vector_share:])

        def load_scale_rows(name, scales, tag, clear):
            window = sb.tile([P, T], U8, name=name, tag=tag)
            clear(window[:].bitcast(I32))
            for quad in range(4):
                nc.sync.dma_start(
                    window[32 * quad : 32 * quad + 4, :].bitcast(I32),
                    scales[0, 4 * quad : 4 * quad + 4, :].bitcast(I32),
                )
            return window

        def load_words(name, words, tag, queue):
            window = sb.tile([P, T], U16, name=name, tag=tag)
            queue.dma_start(window[:].bitcast(I32), words[0].bitcast(I32))
            return window

        def load_row(name, table, row, tag, clear, queue):
            window = sb.tile([P, T], F32, name=name, tag=tag)
            clear(window[:])
            queue.dma_start(window[row : row + 1, :], table[row : row + 1, :])
            return window

        def load_rows(name, rows, tag, queue):
            raw = sb.tile([P, PACK, Q], F32, name=name, tag=tag)
            queue.dma_start(raw[:], rows.rearrange("(p j) w -> p j w", j=PACK))
            return raw

        def round_and_interleave(name, raw, tag):
            grouped = sb.tile([P, Q, PACK], BF16, name=name, tag=tag, align_bytes=64)
            S.activation(grouped[:], raw[:].rearrange("p j w -> p w j"), ACT.Copy)
            return grouped

        def quantise(name, grouped, tag):
            codes = sb.tile([P, Q], U32, name=name + "_codes", tag=tag, align_bytes=64)
            scales = sb.tile([P, Q], U8, name=name + "_scales", align_bytes=64)
            V.quantize_mx(out=codes[:].bitcast(FP8X4), scales=scales[:], in_=grouped[:].rearrange("p w j -> p (w j)"))
            return codes, scales

        def gather(name, window, dtype, tag):
            picked = sb.tile([P, SLOTS], dtype, name=name, tag=tag, align_bytes=64)
            V.tensor_copy(picked[:], window[:].indirect(offsets[:]))
            return picked

        def turn(target, source, blocks):
            for j in blocks:
                PE.transpose(target[:, block(j)], source[:, block(j)], identity[:])

        query_raw = load_rows("query_raw", query, "query_staging", nc.sync)
        key_word_window = load_words("key_word_window", keys_words, "key_word_buffer", nc.sync)
        key_scale_window = load_scale_rows("key_scale_window", keys_scales, "key_scale_buffer", clear_on_gpsimd)
        cv2_window = load_row("cv2_window", cv2, CV2_ROW, "cv2_buffer", lambda w: clear_shared(w, 1280), nc.scalar)
        cv1_window = load_row("cv1_window", cv1, CV1_ROW, "cv1_buffer", lambda w: clear_shared(w, 1024), nc.sync)
        val_scale_window = load_scale_rows("val_scale_window", vals_scales, "val_scale_window", clear_on_vector)
        identity = sb.tile([P, P], F32, name="identity")
        make_identity(nc, identity[:])

        query_grouped = round_and_interleave("query_grouped", query_raw, "query_grouped")
        val_word_window = load_words("val_word_window", vals_words, "query_staging", nc.scalar)

        key_words = gather("key_words", key_word_window, U16, "key_words")
        shyness = sb.tile([P, 1], F32, name="shyness", tag="key_word_buffer")
        nc.sync.dma_start(shyness[:], shy)
        key_scales = gather("key_scales", key_scale_window, U8, "key_scales")
        gout_raw = load_rows("gout_raw", gout, "key_scale_buffer", nc.sync)

        cv2_picked = sb.tile([P, SLOTS], F32, name="cv2_picked", tag="cv2_picked", align_bytes=64)
        S.activation(cv2_picked[:], cv2_window[:].indirect(offsets[:]), ACT.Copy)
        dquery_raw = load_rows("dquery_raw", dquery, "cv2_buffer", nc.scalar)
        cv2_turned = bank("cv2_turned", "bank0")
        turn(cv2_turned, cv2_picked, range(BLOCKS))
        query_codes, query_scales = quantise("query", query_grouped, "query_codes")
        half = SLOTS // 2
        halves = [slice(0, half), slice(half, SLOTS)]
        list_halves = [slice(0, half // 16), slice(half // 16, SLOTS // 16)]
        run_halves = [slice(0, G // 2), slice(G // 2, G)]
        cv1_turned = []
        for h in range(2):
            picked = sb.tile([P, half], F32, name="cv1_picked%d" % h, tag="cv1_picked%d" % h, align_bytes=64)
            S.activation(picked[:], cv1_window[:].indirect(offsets[:, list_halves[h]]), ACT.Copy)
            turned = bank("cv1_turned%d" % h, "bank%d" % (1 + h))
            turn(turned, picked, range(BLOCKS // 2))
            cv1_turned.append(turned)
        base_sb = sb.tile([P, T], F32, name="base_sb", tag="cv1_buffer")
        nc.sync.dma_start(base_sb[:], base)

        a_t = bank("a_t", "bank3")
        for j in range(BLOCKS):
            PE.matmul_mx(
                out=a_t[:, block(j)],
                lhsT=key_words[:, block(j)].bitcast(FP4X4),
                lhsT_scale=key_scales[:, block(j)],
                rhs=query_codes[:].bitcast(FP8X4),
                rhs_scale=query_scales[:],
                start=True,
                stop=True,
            )
        val_scales = gather("val_scales", val_scale_window, U8, "query_grouped")

        def row_major_product(product, codes, scales, words, word_scales):
            PE.matmul_mx(
                out=product,
                lhsT=codes[:].bitcast(FP8X4),
                lhsT_scale=scales[:],
                rhs=words.bitcast(FP4X4),
                rhs_scale=word_scales,
                start=True,
                stop=True,
            )

        u_t = wide("u_t")
        s = bank("s", "bank6")
        for h, cols in enumerate(halves):
            for j in (2 * h, 2 * h + 1):
                c2_j = cv2_turned[:, j * P + CV2_ROW : j * P + CV2_ROW + 1]
                c1_j = cv1_turned[h][:, (j % 2) * P + CV1_ROW : (j % 2) * P + CV1_ROW + 1]
                V.tensor_scalar(u_t[:, block(j)], a_t[:, block(j)], c2_j, c1_j, mult, add)
        for h, cols in enumerate(halves):
            s_t = sb.tile([P, half], F32, name="s_t%d" % h, tag="s_t%d" % h, align_bytes=64)
            V.tensor_tensor(s_t[:], a_t[:, cols], u_t[:, cols], mult)
            turn(s[:, cols], s_t, range(BLOCKS // 2))

        dquery_grouped = round_and_interleave("dquery_grouped", dquery_raw, "cv1_picked0")
        dquery_codes, dquery_scales = quantise("dquery", dquery_grouped, "dquery_codes")
        ta = bank("ta", "bank4")
        row_major_product(ta[:], dquery_codes, dquery_scales, key_words[:], key_scales[:])
        minus_c1 = sb.tile([P, BLOCKS], F32, name="minus_c1")
        for h in range(2):
            S.activation(minus_c1[:, 2 * h : 2 * h + 2], cv1_turned[h][:, CV1_ROW:half:P], ACT.Copy, scale=-1.0)
        e_t = wide("e_t")
        for j in range(BLOCKS):
            S.activation(e_t[:, block(j)], u_t[:, block(j)], ACT.Identity, bias=minus_c1[:, j : j + 1], scale=2.0)
        e = bank("e", "bank7")
        turn(e, e_t, range(BLOCKS))

        val_words = []
        for h in range(2):
            val_words.append(sb.tile([P, half], U16, name="val_words%d" % h, tag="s_t%d" % h, align_bytes=64))
        V.tensor_copy(val_words[0][:], val_word_window[:].indirect(offsets[:, list_halves[0]]))
        minus_max = column("minus_max")
        V.tensor_reduce(minus_max[:], s[:], AXIS.X, ALU.max, negate=True)
        p = wide("p")
        p_sum = column("p_sum")
        S.activation(p[:], s[:], ACT.Exp, bias=minus_max[:], accum_out=p_sum[:])

        V.tensor_copy(val_words[1][:], val_word_window[:].indirect(offsets[:, list_halves[1]]))
        gout_grouped = round_and_interleave("gout_grouped", gout_raw, "cv1_picked1")
        gout_codes, gout_scales = quantise("gout", gout_grouped, "gout_codes")
        c = bank("c", "bank5")
        for h, cols in enumerate(halves):
            row_major_product(c[:, cols], gout_codes, gout_scales, val_words[h][:], val_scales[:, cols])

        minus_shy = column("minus_shy")
        S.activation(minus_shy[:], shyness[:], ACT.Copy, scale=-1.0)

        sums = sb.tile([P, 5, G], F32, name="sums")
        tan, a0, a1, a2, a3 = [sums[:, n, :] for n in range(5)]

        def run_sums_on_gpsimd(name, target, source):
            fours = sb.tile([P, G, 4], F32, name=name + "_fours")
            twos = sb.tile([P, G, 2], F32, name=name + "_twos", tag=name + "_twos")
            nc.gpsimd.tensor_tensor(fours[:], by_run(source)[:, :, 0:4], by_run(source)[:, :, 4:8], add)
            nc.gpsimd.tensor_tensor(twos[:], fours[:, :, 0:2], fours[:, :, 2:4], add)
            nc.gpsimd.tensor_tensor(target, twos[:, :, 0], twos[:, :, 1], add)

        inv_s = column("inv_s")
        p_e = wide("p_e")
        V.tensor_tensor(p_e[:], e[:], p[:], mult)
        V.reciprocal(inv_s[:], p_sum[:])
        run_sums_on_gpsimd("p", a0, p[:])
        nh = column("nh")
        S.activation(nh[:], inv_s[:], ACT.Copy, scale=minus_shy[:])
        k = runs("k")
        S.activation(k[:], a0, ACT.Exp, scale=nh[:])

        two_c2 = sb.tile([P, BLOCKS], F32, name="two_c2")
        S.activation(two_c2[:], cv2_turned[:, CV2_ROW:SLOTS:P], ACT.Copy, scale=2.0)
        e_sq = wide("e_sq")
        S.activation(e_sq[:], e_t[:], ACT.Square)
        q1_t = wide("q1_t")
        for j in range(BLOCKS):
            S.activation(q1_t[:, block(j)], e_sq[:, block(j)], ACT.Identity, bias=two_c2[:, j : j + 1])
        q1 = bank("q1", "bank1")
        turn(q1, q1_t, range(BLOCKS))

        p_sigma, p_c, p_c_sigma, p_q1, p_f = [wide(n) for n in ("p_sigma", "p_c", "p_c_sigma", "p_q1", "p_f")]
        p_sigma_sum, t_mean, r0, r2, inv_u, c_mean = [column(n) for n in ("p_sigma_sum", "t_mean", "r0", "r2", "inv_u", "c_mean")]
        ka = sb.tile([P, 4, G], F32, name="ka")
        r13 = sb.tile([P, 2], F32, name="r13")
        shift = sb.tile([P, 2, G], F32, name="shift")
        V.scalar_tensor_tensor(p_sigma[:], ta[:], 1.0, p_e[:], mult, mult, accum_out=p_sigma_sum[:])
        V.tensor_tensor(p_c[:], c[:], p[:], mult)
        run_sums_on_gpsimd("p_c", a2, p_c[:])
        scattered = sb.tile([P, T], F32, name="scattered", tag="p_c_twos")
        nc.gpsimd.memset(scattered[:], 0.0)
        S.activation(t_mean[:], p_sigma_sum[:], ACT.Copy, scale=inv_s[:])
        V.tensor_tensor(p_c_sigma[:], c[:], p_sigma[:], mult)
        V.tensor_reduce(a1, by_run(p_sigma[:]), AXIS.X, add)
        V.tensor_reduce(a3, by_run(p_c_sigma[:]), AXIS.X, add)
        V.scalar_tensor_tensor(ka[:, 0, :], a0, 1.0, k[:], mult, mult, accum_out=r0[:])
        V.scalar_tensor_tensor(tan, a0, t_mean[:], a1, mult, sub)
        V.scalar_tensor_tensor(ka[:, 2, :], a2, 1.0, k[:], mult, mult, accum_out=r2[:])
        V.reciprocal(inv_u[:], r0[:])
        shares = sb.tile([P, 2, G], F32, name="shares")
        S.activation(shares[:], sums[:, 0:2, :], ACT.Copy, scale=inv_s[:])
        phi = runs("phi")
        S.activation(phi[:], tan, ACT.Copy, scale=nh[:])
        V.scalar_tensor_tensor(shift[:], tan.unsqueeze(1).to_broadcast([P, 2, G]), nh[:], sums[:, 1:4:2, :], mult, mult)
        out_factor, nhf = column("out_factor"), column("nhf")
        S.activation(out_factor[:], inv_u[:], ACT.Copy, scale=-OUT_SCALE)
        kf = runs("kf")
        S.activation(kf[:], k[:], ACT.Copy, scale=out_factor[:])
        S.activation(nhf[:], nh[:], ACT.Copy, scale=out_factor[:])
        V.tensor_tensor(c_mean[:], r2[:], inv_u[:], mult)
        moved = sb.tile([P, 2, G], F32, name="moved")
        V.tensor_tensor(moved[:], sums[:, 2:5:2, :], shift[:], sub)
        yv = sb.tile([P, 2, G], F32, name="yv")
        y0n, v = yv[:, 0, :], yv[:, 1, :]
        V.scalar_tensor_tensor(y0n, ka[:, 0, :], c_mean[:], ka[:, 2, :], mult, sub)
        V.scalar_tensor_tensor(ka[:, 1, :], moved[:, 0, :], 1.0, k[:], mult, mult, accum_out=r13[:, 0:1])
        V.scalar_tensor_tensor(ka[:, 3, :], moved[:, 1, :], 1.0, k[:], mult, mult, accum_out=r13[:, 1:2])
        mn = column("mn")
        mn_terms = runs("mn_terms")
        V.scalar_tensor_tensor(mn_terms[:], y0n, nhf[:], shares[:, 1, :], mult, mult, accum_out=mn[:])
        zr = sb.tile([P, 2], F32, name="zr")
        V.tensor_tensor(zr[:], r13[:], inv_u[:].to_broadcast([P, 2]), mult)
        z = zr[:, 0:1]
        y1n = runs("y1n")
        V.scalar_tensor_tensor(y1n[:], ka[:, 1, :], c_mean[:], ka[:, 3, :], mult, sub)
        zt = column("zt")
        V.tensor_tensor(zt[:], z, t_mean[:], add)
        ntc = column("ntc")
        V.scalar_tensor_tensor(ntc[:], c_mean[:], z, zr[:, 1:2], mult, sub)
        ktc = runs("ktc")
        S.activation(ktc[:], kf[:], ACT.Copy, scale=ntc[:])
        v1 = runs("v1")
        V.scalar_tensor_tensor(v1[:], y0n, zt[:], y1n[:], mult, sub)
        V.scalar_tensor_tensor(v, ka[:, 0, :], ntc[:], v1[:], mult, add)
        n_terms = sb.tile([P, 2, G], F32, name="n_terms")
        n_sum = column("n_sum")
        V.scalar_tensor_tensor(n_terms[:], yv[:], nhf[:], shares[:], mult, mult, accum_out=n_sum[:])
        dd = runs("dd")
        V.scalar_tensor_tensor(dd[:], v, nhf[:], ktc[:], mult, add)

        x1, x2, x3, x4, x5, x6 = [wide("x%d" % n) for n in range(1, 7)]

        def spread_half(ap, gs):
            return ap[:, gs].unsqueeze(2).to_broadcast([P, G // 2, RUN])

        for cols in halves:
            V.tensor_tensor(p_q1[:, cols], q1[:, cols], p[:, cols], mult)
        for cols in halves:
            V.tensor_tensor(p_f[:, cols], ta[:, cols], p_q1[:, cols], mult)
        for cols, gs in zip(halves, run_halves):
            V.scalar_tensor_tensor(by_run(x1[:, cols]), by_run(c[:, cols]), c_mean[:], spread_half(kf, gs), sub, mult)
        for cols, gs in zip(halves, run_halves):
            V.scalar_tensor_tensor(by_run(x2[:, cols]), spread_half(y0n, gs), nhf[:], by_run(x1[:, cols]), mult, sub)
        for cols, gs in zip(halves, run_halves):
            V.scalar_tensor_tensor(by_run(x4[:, cols]), spread_half(phi, gs), z, by_run(x1[:, cols]), add, mult)
        for cols in halves:
            V.scalar_tensor_tensor(x3[:, cols], x2[:, cols], mn[:], p_f[:, cols], sub, mult)
        for cols, gs in zip(halves, run_halves):
            V.scalar_tensor_tensor(
                by_run(x5[:, cols]), by_run(x4[:, cols]), n_sum[:], spread_half(dd, gs), add, sub
            )
        for cols in halves:
            V.tensor_tensor(x6[:, cols], p_e[:, cols], x5[:, cols], mult)
        V.tensor_tensor(scattered[:].indirect(offsets[:]), x3[:], x6[:], add)

        first = 0
        for n, width in enumerate(STORE_WIDTHS):
            cols = slice(first, first + width)
            result = sb.tile([P, width], F32, name="result%d" % n)
            V.tensor_tensor(result[:], scattered[:, cols], base_sb[:, cols], add)
            queue = nc.sync if n % 2 == 0 else nc.scalar
            queue.dma_start(out[:, cols], result[:])
            first += width
